import numpy as np
import ml_dtypes


def mxq(x, axis, fmt="e4m3"):
    dtype, down = {"e4m3": (ml_dtypes.float8_e4m3fn, 7), "e5m2": (ml_dtypes.float8_e5m2, 14)}[fmt]
    v = np.moveaxis(np.asarray(x, np.float32).astype(ml_dtypes.bfloat16).astype(np.float64), axis, -1)
    blocks = v.reshape(v.shape[:-1] + (-1, 32))
    amax = np.abs(blocks).max(-1, keepdims=True)
    byte = np.maximum(np.where(amax > 0, np.frexp(amax)[1] - 1 + 127, 0) - down, 1)
    scale = np.exp2(byte - 127.0)
    codes = (blocks / scale).astype(np.float32).astype(dtype).astype(np.float64)
    return np.moveaxis((codes * scale).reshape(v.shape), -1, axis)


WIDE = False


def mx_kscale(k):
    if not WIDE:
        return np.ones(k)
    levels = np.array([10, -10, 5, -5, 0])
    if k % 512:
        return np.exp2(np.random.permutation(np.resize(levels, k // 32))).repeat(32)
    a = np.empty((k // 512, 16))
    for p in range(k // 512):
        a[p, :8] = np.random.permutation(np.resize(levels, 8))
        for g in range(8):
            far = levels[np.abs(levels - a[p, g]) >= 10]
            a[p, g + 8] = far[np.random.randint(len(far))]
    return np.exp2(a.ravel()).repeat(32)


def f64(x):
    return np.asarray(x).astype(np.float64)


def striped8(idx):
    return np.asarray(idx).reshape(8, -1, 16).transpose(0, 2, 1).reshape(128, -1).astype(np.uint16)


def unstriped8(offs):
    return offs.reshape(8, 16, -1).transpose(0, 2, 1).reshape(8, -1).astype(np.int64)


def pick8(x, idx, run):
    r = np.arange(len(x))
    return x[r[:, None], idx[r % (8 * run) // run]]


E2M1 = np.array([0.0, 0.5, 1.0, 1.5, 2.0, 3.0, 4.0, 6.0, -0.0, -0.5, -1.0, -1.5, -2.0, -3.0, -4.0, -6.0])


def pack_weight(w, fmt):
    k, n = w.shape
    w = f64(np.asarray(w, np.float32).astype(ml_dtypes.bfloat16)).reshape(k // 32, 32, n)
    amax = np.abs(w).max(1)
    if fmt == "e4m3":
        byte = np.frexp(amax)[1] - 1 + 127 - 7
    else:
        mant, ex = np.frexp(amax / 6.0)
        byte = np.where(mant > 0.5, ex, ex - 1) + 127
    byte = np.clip(np.where(amax > 0, byte, 1), 1, 254)
    scaled = (w * np.exp2(127.0 - byte)[:, None, :]).reshape(k, n).astype(np.float32)
    by_word = np.ascontiguousarray(scaled.reshape(k // 512, 128, 4, n).transpose(0, 1, 3, 2))
    if fmt == "e4m3":
        words = by_word.astype(ml_dtypes.float8_e4m3fn).view(np.uint8)
    else:
        c = by_word.astype(ml_dtypes.float4_e2m1fn).view(np.uint8) & 0xF
        words = (c[..., 0::2] | (c[..., 1::2] << 4)).reshape(k // 512, 128, 2 * n)
    return np.ascontiguousarray(words), np.ascontiguousarray(byte.astype(np.uint8).reshape(k // 512, 16, n))


def unpack_weight(words, scales, fmt):
    g, _, n = scales.shape
    words = np.ascontiguousarray(words).reshape(g, 128, n, -1)
    if fmt == "e4m3":
        vals = words.view(ml_dtypes.float8_e4m3fn).astype(np.float64)
    else:
        nib = np.empty((g, 128, n, 4), np.uint8)
        nib[..., 0::2] = words & 0xF
        nib[..., 1::2] = words >> 4
        vals = E2M1[nib]
    vals = vals * np.repeat(np.exp2(scales.astype(np.float64) - 127.0), 8, axis=1)[..., None]
    return vals.transpose(0, 1, 3, 2).reshape(g * 512, n)


D, T, I, Q = 512, 1024, 512, 128


def setup_inputs():
    n = np.random.standard_normal
    idx = np.stack([np.random.permutation(T)[:I] for _ in range(8)])
    idx2 = np.stack([np.random.permutation(T)[:I] for _ in range(8)])
    idx3 = np.stack([np.random.permutation(T)[:I] for _ in range(8)])
    fd = mx_kscale(D)
    keysp = pack_weight(n((D, T)) / fd[:, None], "e2m1")
    return {
        "query": (n((D, Q)) * 0.9 / np.sqrt(D) * fd[:, None]).astype(np.float32),
        "query2": (n((D, Q)) * 0.9 / np.sqrt(D) * fd[:, None]).astype(np.float32),
        "keys_words": keysp[0],
        "keys_scales": keysp[1],
        "lam": (np.random.uniform(1.0, 2.5, (Q, 1))).astype(np.float32),
        "lean": (np.random.uniform(0.2, 0.6, (Q, 1))).astype(np.float32),
        "base": (0.3 * n((Q, I))).astype(np.float32),
        "gain2": (np.random.uniform(0.5, 2.0, (Q, 1))).astype(np.float32),
        "offs": striped8(idx),
        "offs2": striped8(idx2),
        "offs3": striped8(idx3),
    }


def reference(query, query2, keys_words, keys_scales, lam, lean, base, gain2, offs, offs2, offs3):
    idx = unstriped8(offs)
    idx2 = unstriped8(offs2)
    idx3 = unstriped8(offs3)
    keysu = unpack_weight(keys_words, keys_scales, "e2m1")
    queryq = mxq(f64(query), 0, "e4m3")
    a = queryq.T @ keysu
    query2q = mxq(f64(query2), 0, "e4m3")
    b = query2q.T @ keysu
    e1s = np.exp(pick8(a, idx, 16))
    s = e1s / (e1s + np.exp(pick8(a, idx2, 16)) + np.exp(pick8(b, idx3, 16))) * f64(lam)
    p = np.exp(s - np.max(s, axis=1, keepdims=True))
    r = p / np.sum(p, axis=1, keepdims=True)
    m0 = np.sum(r * s, axis=1, keepdims=True)
    w = r * ((s - m0) * f64(lean) + 1.0)
    y = np.tanh(w * f64(gain2) * 128.0) + f64(base)
    return y

@@ -1,0 +1,167 @@
+from contextlib import ExitStack
+
+import concourse.mybir as mybir
+
+D, T, SLOTS, Q = 512, 1024, 512, 128
+FLOPS = 2 * 2 * D * T * Q
+
+F32 = mybir.dt.float32
+BF16 = mybir.dt.bfloat16
+I32 = mybir.dt.int32
+U32 = mybir.dt.uint32
+U16 = mybir.dt.uint16
+U8 = mybir.dt.uint8
+FP8X4 = mybir.dt.float8_e4m3fn_x4
+FP4X4 = mybir.dt.float4_e2m1fn_x4
+ALU = mybir.AluOpType
+ACT = mybir.ActivationFunctionType
+AXIS = mybir.AxisListType
+
+P = 128
+PACK = 4
+BANK = 512
+HALF = SLOTS // 2
+LIST_HALF = HALF // 16
+
+
+def tile_attend_quotaratio_leaning_gated_heads_kernel(
+    tc, query, query2, keys_words, keys_scales, lam, lean, base, gain2, offs, offs2, offs3, out
+):
+    nc = tc.nc
+    with ExitStack() as ctx:
+        sb = ctx.enter_context(tc.tile_pool(name="sb", bufs=1))
+        psum = ctx.enter_context(tc.psum_pool(name="psum", bufs=1))
+
+        def f32_tile(name, width):
+            return sb.tile([P, width], F32, name=name, align_bytes=64)
+
+        list1 = sb.tile([P, SLOTS // 16], U16, name="list1")
+        list2 = sb.tile([P, SLOTS // 16], U16, name="list2")
+        list3 = sb.tile([P, SLOTS // 16], U16, name="list3")
+        qa_raw = sb.tile([P, PACK, Q], F32, name="qa_raw", align_bytes=64)
+        qb_raw = sb.tile([P, PACK, Q], F32, name="qb_raw", align_bytes=64)
+        key_words = sb.tile([P, 2 * T], U8, name="key_words", align_bytes=64)
+        key_scales = sb.tile([P, T], U8, name="key_scales", align_bytes=64)
+        lam_sb = f32_tile("lam_sb", 1)
+        lean_sb = f32_tile("lean_sb", 1)
+        gain_sb = f32_tile("gain_sb", 1)
+        base_sb = f32_tile("base_sb", SLOTS)
+
+        nc.vector.memset(key_scales[:].bitcast(I32), 0)
+        nc.sync.dma_start(out=qa_raw[:], in_=query.rearrange("(p j) q -> p j q", j=PACK))
+        nc.sync.dma_start(out=key_words[:].bitcast(I32), in_=keys_words[0].bitcast(I32))
+        for quad in range(4):
+            nc.scalar.dma_start(
+                out=key_scales[32 * quad : 32 * quad + 4, :].bitcast(I32),
+                in_=keys_scales[0, 4 * quad : 4 * quad + 4, :].bitcast(I32),
+            )
+        nc.sync.dma_start(out=qb_raw[:], in_=query2.rearrange("(p j) q -> p j q", j=PACK))
+        nc.sync.dma_start(list1[:], offs)
+        nc.sync.dma_start(list2[:], offs2)
+        nc.sync.dma_start(list3[:], offs3)
+        nc.gpsimd.dma_start(out=lam_sb[:], in_=lam)
+        nc.gpsimd.dma_start(out=lean_sb[:], in_=lean)
+        nc.gpsimd.dma_start(out=gain_sb[:], in_=gain2)
+        nc.sync.dma_start(out=base_sb[:], in_=base)
+
+        qa_bf = sb.tile([P, Q, PACK], BF16, name="qa_bf", align_bytes=64)
+        qb_bf = sb.tile([P, Q, PACK], BF16, name="qb_bf", align_bytes=64)
+        qa_codes = sb.tile([P, Q], U32, name="qa_codes", align_bytes=64)
+        qb_codes = sb.tile([P, Q], U32, name="qb_codes", align_bytes=64)
+        qa_scales = sb.tile([P, Q], U8, name="qa_scales", align_bytes=64)
+        qb_scales = sb.tile([P, Q], U8, name="qb_scales", align_bytes=64)
+
+        def quantise(codes, scales, grouped):
+            nc.vector.quantize_mx(
+                out=codes[:].bitcast(FP8X4),
+                scales=scales[:],
+                in_=grouped[:].rearrange("p q j -> p (q j)"),
+            )
+
+        def scores(name, codes, scales):
+            banks = []
+            for h in range(T // BANK):
+                bank = psum.tile([P, BANK], F32, name=f"{name}{h}")
+                nc.tensor.matmul_mx(
+                    out=bank[:],
+                    lhsT=codes[:].bitcast(FP8X4),
+                    lhsT_scale=scales[:],
+                    rhs=key_words[:, 2 * BANK * h : 2 * BANK * (h + 1)].bitcast(FP4X4),
+                    rhs_scale=key_scales[:, BANK * h : BANK * (h + 1)],
+                    start=True,
+                    stop=True,
+                )
+                banks.append(bank)
+            return banks
+
+        nc.vector.tensor_copy(out=qa_bf[:], in_=qa_raw[:].rearrange("p j q -> p q j"))
+        quantise(qa_codes, qa_scales, qa_bf)
+        a_banks = scores("a_bank", qa_codes, qa_scales)
+        nc.scalar.copy(out=qb_bf[:], in_=qb_raw[:].rearrange("p j q -> p q j"))
+        quantise(qb_codes, qb_scales, qb_bf)
+        b_banks = scores("b_bank", qb_codes, qb_scales)
+
+        a_sb = f32_tile("a_sb", T)
+        b_sb = f32_tile("b_sb", T)
+        nc.vector.tensor_copy(out=a_sb[:, :BANK], in_=a_banks[0][:])
+        nc.scalar.copy(out=a_sb[:, BANK:], in_=a_banks[1][:])
+
+        cols = [slice(0, HALF), slice(HALF, SLOTS)]
+        ents = [slice(0, LIST_HALF), slice(LIST_HALF, 2 * LIST_HALF)]
+
+        a1 = f32_tile("a1", SLOTS)
+        d2 = f32_tile("d2", SLOTS)
+        d3 = f32_tile("d3", SLOTS)
+        x2 = f32_tile("x2", SLOTS)
+        x3 = f32_tile("x3", SLOTS)
+        den = f32_tile("den", SLOTS)
+        nc.vector.tensor_copy(out=a1[:, cols[0]], in_=a_sb[:].indirect(list1[:, ents[0]]))
+        nc.scalar.activation(a1[:, cols[1]], a_sb[:].indirect(list1[:, ents[1]]), ACT.Copy)
+        for h in range(T // BANK):
+            nc.scalar.copy(out=b_sb[:, BANK * h : BANK * (h + 1)], in_=b_banks[h][:])
+        for h in range(2):
+            nc.vector.tensor_tensor(d2[:, cols[h]], a_sb[:].indirect(list2[:, ents[h]]), a1[:, cols[h]], ALU.subtract)
+        nc.scalar.activation(x2[:], d2[:], ACT.Exp)
+        for h in range(2):
+            nc.vector.tensor_tensor(d3[:, cols[h]], b_sb[:].indirect(list3[:, ents[h]]), a1[:, cols[h]], ALU.subtract)
+            nc.scalar.activation(x3[:, cols[h]], d3[:, cols[h]], ACT.Exp)
+        for h in range(2):
+            nc.vector.scalar_tensor_tensor(
+                den[:, cols[h]], x2[:, cols[h]], 1.0, x3[:, cols[h]], ALU.add, ALU.add
+            )
+
+        root = f32_tile("root", SLOTS)
+        s = f32_tile("s", SLOTS)
+        for h in range(2):
+            nc.scalar.activation(root[:, cols[h]], den[:, cols[h]], ACT.Abs_reciprocal_sqrt)
+            nc.vector.scalar_tensor_tensor(
+                s[:, cols[h]], root[:, cols[h]], lam_sb[:], root[:, cols[h]], ALU.mult, ALU.mult
+            )
+        neg_max = f32_tile("neg_max", 1)
+        nc.vector.tensor_reduce(neg_max[:], s[:], AXIS.X, ALU.max, negate=True)
+
+        p = f32_tile("p", SLOTS)
+        p_sum = f32_tile("p_sum", 1)
+        nc.scalar.activation(p[:], s[:], ACT.Exp, bias=neg_max[:], accum_out=p_sum[:])
+
+        psl = f32_tile("psl", SLOTS)
+        psl_sum = f32_tile("psl_sum", 1)
+        inv_sum = f32_tile("inv_sum", 1)
+        shift = f32_tile("shift", 1)
+        neg_gain = f32_tile("neg_gain", 1)
+        nc.vector.reciprocal(inv_sum[:], p_sum[:])
+        nc.vector.scalar_tensor_tensor(psl[:], s[:], lean_sb[:], p[:], ALU.mult, ALU.mult, accum_out=psl_sum[:])
+        nc.vector.tensor_scalar(neg_gain[:], gain_sb[:], inv_sum[:], -128.0, ALU.mult, ALU.mult)
+        nc.vector.tensor_scalar(shift[:], psl_sum[:], inv_sum[:], 1.0, ALU.mult, ALU.subtract)
+
+        neg_w = f32_tile("neg_w", SLOTS)
+        gate = f32_tile("gate", SLOTS)
+        result = f32_tile("result", SLOTS)
+        for h in range(2):
+            nc.vector.scalar_tensor_tensor(
+                neg_w[:, cols[h]], p[:, cols[h]], shift[:], psl[:, cols[h]], ALU.mult, ALU.subtract
+            )
+            nc.scalar.activation(gate[:, cols[h]], neg_w[:, cols[h]], ACT.Tanh, scale=neg_gain[:])
+        for h in range(2):
+            nc.vector.tensor_tensor(result[:, cols[h]], gate[:, cols[h]], base_sb[:, cols[h]], ALU.add)
+            nc.sync.dma_start(out=out[:, cols[h]], in_=result[:, cols[h]])

@@ -40,28 +40,35 @@ def tile_attend_quotaratio_leaning_gated_heads_kernel(
         list3 = sb.tile([P, SLOTS // 16], U16, name="list3")
         qa_raw = sb.tile([P, PACK, Q], F32, name="qa_raw", align_bytes=64)
         qb_raw = sb.tile([P, PACK, Q], F32, name="qb_raw", align_bytes=64)
-        key_words = sb.tile([P, 2 * T], U8, name="key_words", align_bytes=64)
+        key_words = [sb.tile([P, 2 * BANK], U8, name=f"key_words{h}", align_bytes=64) for h in range(2)]
         key_scales = sb.tile([P, T], U8, name="key_scales", align_bytes=64)
         lam_sb = f32_tile("lam_sb", 1)
         lean_sb = f32_tile("lean_sb", 1)
         gain_sb = f32_tile("gain_sb", 1)
         base_sb = f32_tile("base_sb", SLOTS)
 
+        def load_key_words(h):
+            nc.sync.dma_start(
+                out=key_words[h][:].bitcast(I32),
+                in_=keys_words[0, :, 2 * BANK * h : 2 * BANK * (h + 1)].bitcast(I32),
+            )
+
         nc.vector.memset(key_scales[:].bitcast(I32), 0)
         nc.sync.dma_start(out=qa_raw[:], in_=query.rearrange("(p j) q -> p j q", j=PACK))
-        nc.sync.dma_start(out=key_words[:].bitcast(I32), in_=keys_words[0].bitcast(I32))
+        load_key_words(0)
         for quad in range(4):
-            nc.scalar.dma_start(
+            nc.sync.dma_start(
                 out=key_scales[32 * quad : 32 * quad + 4, :].bitcast(I32),
                 in_=keys_scales[0, 4 * quad : 4 * quad + 4, :].bitcast(I32),
             )
+        load_key_words(1)
         nc.sync.dma_start(out=qb_raw[:], in_=query2.rearrange("(p j) q -> p j q", j=PACK))
         nc.sync.dma_start(list1[:], offs)
         nc.sync.dma_start(list2[:], offs2)
         nc.sync.dma_start(list3[:], offs3)
-        nc.gpsimd.dma_start(out=lam_sb[:], in_=lam)
-        nc.gpsimd.dma_start(out=lean_sb[:], in_=lean)
-        nc.gpsimd.dma_start(out=gain_sb[:], in_=gain2)
+        nc.sync.dma_start(out=lam_sb[:], in_=lam)
+        nc.sync.dma_start(out=lean_sb[:], in_=lean)
+        nc.sync.dma_start(out=gain_sb[:], in_=gain2)
         nc.sync.dma_start(out=base_sb[:], in_=base)
 
         qa_bf = sb.tile([P, Q, PACK], BF16, name="qa_bf", align_bytes=64)
@@ -78,33 +85,43 @@ def tile_attend_quotaratio_leaning_gated_heads_kernel(
                 in_=grouped[:].rearrange("p q j -> p (q j)"),
             )
 
-        def scores(name, codes, scales):
+        def interleave(grouped, raw):
+            nc.vector.tensor_copy(out=grouped[:, :80, :], in_=raw[:, :, :80].rearrange("p j q -> p q j"))
+            nc.scalar.copy(out=grouped[:, 80:, :], in_=raw[:, :, 80:].rearrange("p j q -> p q j"))
+
+        def scores(name, codes, scales, width):
             banks = []
-            for h in range(T // BANK):
-                bank = psum.tile([P, BANK], F32, name=f"{name}{h}")
+            for t0 in range(0, T, width):
+                bank = psum.tile([P, width], F32, name=f"{name}{t0}")
+                c0 = t0 % BANK
                 nc.tensor.matmul_mx(
                     out=bank[:],
                     lhsT=codes[:].bitcast(FP8X4),
                     lhsT_scale=scales[:],
-                    rhs=key_words[:, 2 * BANK * h : 2 * BANK * (h + 1)].bitcast(FP4X4),
-                    rhs_scale=key_scales[:, BANK * h : BANK * (h + 1)],
+                    rhs=key_words[t0 // BANK][:, 2 * c0 : 2 * (c0 + width)].bitcast(FP4X4),
+                    rhs_scale=key_scales[:, t0 : t0 + width],
                     start=True,
                     stop=True,
                 )
                 banks.append(bank)
             return banks
 
-        nc.vector.tensor_copy(out=qa_bf[:], in_=qa_raw[:].rearrange("p j q -> p q j"))
+        A_WIDTH = 256
+        interleave(qa_bf, qa_raw)
         quantise(qa_codes, qa_scales, qa_bf)
-        a_banks = scores("a_bank", qa_codes, qa_scales)
-        nc.scalar.copy(out=qb_bf[:], in_=qb_raw[:].rearrange("p j q -> p q j"))
+        a_banks = scores("a_bank", qa_codes, qa_scales, A_WIDTH)
+        interleave(qb_bf, qb_raw)
         quantise(qb_codes, qb_scales, qb_bf)
-        b_banks = scores("b_bank", qb_codes, qb_scales)
+        b_banks = scores("b_bank", qb_codes, qb_scales, BANK)
 
         a_sb = f32_tile("a_sb", T)
         b_sb = f32_tile("b_sb", T)
-        nc.vector.tensor_copy(out=a_sb[:, :BANK], in_=a_banks[0][:])
-        nc.scalar.copy(out=a_sb[:, BANK:], in_=a_banks[1][:])
+        for k, bank in enumerate(a_banks):
+            dst = a_sb[:, A_WIDTH * k : A_WIDTH * (k + 1)]
+            if k % 2 == 0:
+                nc.vector.tensor_copy(out=dst, in_=bank[:])
+            else:
+                nc.scalar.copy(out=dst, in_=bank[:])
 
         cols = [slice(0, HALF), slice(HALF, SLOTS)]
         ents = [slice(0, LIST_HALF), slice(LIST_HALF, 2 * LIST_HALF)]
@@ -119,7 +136,7 @@ def tile_attend_quotaratio_leaning_gated_heads_kernel(
         nc.scalar.activation(a1[:, cols[1]], a_sb[:].indirect(list1[:, ents[1]]), ACT.Copy)
         for h in range(T // BANK):
             nc.scalar.copy(out=b_sb[:, BANK * h : BANK * (h + 1)], in_=b_banks[h][:])
-        for h in range(2):
+        for h in (1, 0):
             nc.vector.tensor_tensor(d2[:, cols[h]], a_sb[:].indirect(list2[:, ents[h]]), a1[:, cols[h]], ALU.subtract)
         nc.scalar.activation(x2[:], d2[:], ACT.Exp)
         for h in range(2):
@@ -140,6 +157,11 @@ def tile_attend_quotaratio_leaning_gated_heads_kernel(
         neg_max = f32_tile("neg_max", 1)
         nc.vector.tensor_reduce(neg_max[:], s[:], AXIS.X, ALU.max, negate=True)
 
+        lean_s = f32_tile("lean_s", SLOTS)
+        gain128 = f32_tile("gain128", 1)
+        nc.vector.tensor_scalar(lean_s[:], s[:], lean_sb[:], 1.0, ALU.mult, ALU.add)
+        nc.vector.tensor_scalar(gain128[:], gain_sb[:], 128.0, None, ALU.mult)
+
         p = f32_tile("p", SLOTS)
         p_sum = f32_tile("p_sum", 1)
         nc.scalar.activation(p[:], s[:], ACT.Exp, bias=neg_max[:], accum_out=p_sum[:])
@@ -147,21 +169,23 @@ def tile_attend_quotaratio_leaning_gated_heads_kernel(
         psl = f32_tile("psl", SLOTS)
         psl_sum = f32_tile("psl_sum", 1)
         inv_sum = f32_tile("inv_sum", 1)
-        shift = f32_tile("shift", 1)
-        neg_gain = f32_tile("neg_gain", 1)
+        factor = f32_tile("factor", 1)
+        scaled = f32_tile("scaled", SLOTS)
+        nc.scalar.activation(scaled[:], lean_s[:], ACT.Copy, scale=p_sum[:])
         nc.vector.reciprocal(inv_sum[:], p_sum[:])
         nc.vector.scalar_tensor_tensor(psl[:], s[:], lean_sb[:], p[:], ALU.mult, ALU.mult, accum_out=psl_sum[:])
-        nc.vector.tensor_scalar(neg_gain[:], gain_sb[:], inv_sum[:], -128.0, ALU.mult, ALU.mult)
-        nc.vector.tensor_scalar(shift[:], psl_sum[:], inv_sum[:], 1.0, ALU.mult, ALU.subtract)
+        nc.vector.tensor_scalar(factor[:], inv_sum[:], inv_sum[:], gain128[:], ALU.mult, ALU.mult)
 
-        neg_w = f32_tile("neg_w", SLOTS)
+        w = f32_tile("w", SLOTS)
         gate = f32_tile("gate", SLOTS)
         result = f32_tile("result", SLOTS)
-        for h in range(2):
-            nc.vector.scalar_tensor_tensor(
-                neg_w[:, cols[h]], p[:, cols[h]], shift[:], psl[:, cols[h]], ALU.mult, ALU.subtract
-            )
-            nc.scalar.activation(gate[:, cols[h]], neg_w[:, cols[h]], ACT.Tanh, scale=neg_gain[:])
-        for h in range(2):
-            nc.vector.tensor_tensor(result[:, cols[h]], gate[:, cols[h]], base_sb[:, cols[h]], ALU.add)
-            nc.sync.dma_start(out=out[:, cols[h]], in_=result[:, cols[h]])
+        CH = 128
+        chunks = [slice(c, c + CH) for c in range(0, SLOTS, CH)]
+        for c in chunks:
+            nc.vector.scalar_tensor_tensor(w[:, c], scaled[:, c], psl_sum[:], p[:, c], ALU.subtract, ALU.mult)
+            nc.scalar.activation(gate[:, c], w[:, c], ACT.Tanh, scale=factor[:])
+        for k, c in enumerate(chunks):
+            nc.vector.tensor_tensor(result[:, c], gate[:, c], base_sb[:, c], ALU.add)
+            if k >= 1:
+                st = slice(0, 2 * CH) if k == 1 else c
+                nc.sync.dma_start(out=out[:, st], in_=result[:, st])

@@ -15,13 +15,18 @@ FP8X4 = mybir.dt.float8_e4m3fn_x4
 FP4X4 = mybir.dt.float4_e2m1fn_x4
 ALU = mybir.AluOpType
 ACT = mybir.ActivationFunctionType
-AXIS = mybir.AxisListType
 
 P = 128
 PACK = 4
+QUADRANT = 32
+SCALE_ROWS = 4
+GROUP = 16
 BANK = 512
+QUARTER = T // 4
 HALF = SLOTS // 2
-LIST_HALF = HALF // 16
+VECTOR_QUERIES = 80
+RECIPROCAL_SLOTS = 128
+CHUNK = 128
 
 
 def tile_attend_quotaratio_leaning_gated_heads_kernel(
@@ -35,33 +40,26 @@ def tile_attend_quotaratio_leaning_gated_heads_kernel(
         def f32_tile(name, width):
             return sb.tile([P, width], F32, name=name, align_bytes=64)
 
-        list1 = sb.tile([P, SLOTS // 16], U16, name="list1")
-        list2 = sb.tile([P, SLOTS // 16], U16, name="list2")
-        list3 = sb.tile([P, SLOTS // 16], U16, name="list3")
+        list1 = sb.tile([P, SLOTS // GROUP], U16, name="list1")
+        list2 = sb.tile([P, SLOTS // GROUP], U16, name="list2")
+        list3 = sb.tile([P, SLOTS // GROUP], U16, name="list3")
         qa_raw = sb.tile([P, PACK, Q], F32, name="qa_raw", align_bytes=64)
-        qb_raw = sb.tile([P, PACK, Q], F32, name="qb_raw", align_bytes=64)
-        key_words = [sb.tile([P, 2 * BANK], U8, name=f"key_words{h}", align_bytes=64) for h in range(2)]
+        qb_raw = sb.tile([P, PACK, Q], F32, name="qb_raw", tag="qb_then_a", align_bytes=64)
+        key_words = sb.tile([P, 2 * T], U8, name="key_words", align_bytes=64)
         key_scales = sb.tile([P, T], U8, name="key_scales", align_bytes=64)
         lam_sb = f32_tile("lam_sb", 1)
         lean_sb = f32_tile("lean_sb", 1)
         gain_sb = f32_tile("gain_sb", 1)
         base_sb = f32_tile("base_sb", SLOTS)
 
-        def load_key_words(h):
-            nc.sync.dma_start(
-                out=key_words[h][:].bitcast(I32),
-                in_=keys_words[0, :, 2 * BANK * h : 2 * BANK * (h + 1)].bitcast(I32),
-            )
-
         nc.vector.memset(key_scales[:].bitcast(I32), 0)
         nc.sync.dma_start(out=qa_raw[:], in_=query.rearrange("(p j) q -> p j q", j=PACK))
-        load_key_words(0)
-        for quad in range(4):
+        nc.sync.dma_start(out=key_words[:].bitcast(I32), in_=keys_words[0].bitcast(I32))
+        for quad in range(P // QUADRANT):
             nc.sync.dma_start(
-                out=key_scales[32 * quad : 32 * quad + 4, :].bitcast(I32),
-                in_=keys_scales[0, 4 * quad : 4 * quad + 4, :].bitcast(I32),
+                out=key_scales[QUADRANT * quad : QUADRANT * quad + SCALE_ROWS, :].bitcast(I32),
+                in_=keys_scales[0, SCALE_ROWS * quad : SCALE_ROWS * (quad + 1), :].bitcast(I32),
             )
-        load_key_words(1)
         nc.sync.dma_start(out=qb_raw[:], in_=query2.rearrange("(p j) q -> p j q", j=PACK))
         nc.sync.dma_start(list1[:], offs)
         nc.sync.dma_start(list2[:], offs2)
@@ -78,6 +76,11 @@ def tile_attend_quotaratio_leaning_gated_heads_kernel(
         qa_scales = sb.tile([P, Q], U8, name="qa_scales", align_bytes=64)
         qb_scales = sb.tile([P, Q], U8, name="qb_scales", align_bytes=64)
 
+        def round_and_interleave(grouped, raw):
+            first, rest = slice(0, VECTOR_QUERIES), slice(VECTOR_QUERIES, Q)
+            nc.vector.tensor_copy(out=grouped[:, first, :], in_=raw[:, :, first].rearrange("p j q -> p q j"))
+            nc.scalar.copy(out=grouped[:, rest, :], in_=raw[:, :, rest].rearrange("p j q -> p q j"))
+
         def quantise(codes, scales, grouped):
             nc.vector.quantize_mx(
                 out=codes[:].bitcast(FP8X4),
@@ -85,46 +88,44 @@ def tile_attend_quotaratio_leaning_gated_heads_kernel(
                 in_=grouped[:].rearrange("p q j -> p (q j)"),
             )
 
-        def interleave(grouped, raw):
-            nc.vector.tensor_copy(out=grouped[:, :80, :], in_=raw[:, :, :80].rearrange("p j q -> p q j"))
-            nc.scalar.copy(out=grouped[:, 80:, :], in_=raw[:, :, 80:].rearrange("p j q -> p q j"))
+        def score_pass(bank, codes, scales, t0):
+            width = bank.shape[1]
+            nc.tensor.matmul_mx(
+                out=bank,
+                lhsT=codes[:].bitcast(FP8X4),
+                lhsT_scale=scales[:],
+                rhs=key_words[:, 2 * t0 : 2 * (t0 + width)].bitcast(FP4X4),
+                rhs_scale=key_scales[:, t0 : t0 + width],
+                start=True,
+                stop=True,
+            )
 
-        def scores(name, codes, scales, width):
-            banks = []
-            for t0 in range(0, T, width):
-                bank = psum.tile([P, width], F32, name=f"{name}{t0}")
-                c0 = t0 % BANK
-                nc.tensor.matmul_mx(
-                    out=bank[:],
-                    lhsT=codes[:].bitcast(FP8X4),
-                    lhsT_scale=scales[:],
-                    rhs=key_words[t0 // BANK][:, 2 * c0 : 2 * (c0 + width)].bitcast(FP4X4),
-                    rhs_scale=key_scales[:, t0 : t0 + width],
-                    start=True,
-                    stop=True,
-                )
-                banks.append(bank)
-            return banks
-
-        A_WIDTH = 256
-        interleave(qa_bf, qa_raw)
+        round_and_interleave(qa_bf, qa_raw)
         quantise(qa_codes, qa_scales, qa_bf)
-        a_banks = scores("a_bank", qa_codes, qa_scales, A_WIDTH)
-        interleave(qb_bf, qb_raw)
+        a_head = psum.tile([P, 2 * QUARTER], F32, name="a_head")
+        a_mid = psum.tile([P, QUARTER], F32, name="a_mid")
+        a_tail = psum.tile([P, 2 * BANK], F32, name="a_tail", tag="a_then_b")
+        score_pass(a_head[:], qa_codes, qa_scales, 0)
+        score_pass(a_mid[:], qa_codes, qa_scales, 2 * QUARTER)
+        score_pass(a_tail[:, :QUARTER], qa_codes, qa_scales, 3 * QUARTER)
+        round_and_interleave(qb_bf, qb_raw)
         quantise(qb_codes, qb_scales, qb_bf)
-        b_banks = scores("b_bank", qb_codes, qb_scales, BANK)
+        b_head = psum.tile([P, QUARTER], F32, name="b_head")
+        score_pass(b_head[:], qb_codes, qb_scales, 0)
 
-        a_sb = f32_tile("a_sb", T)
+        a_sb = sb.tile([P, T], F32, name="a_sb", tag="qb_then_a", align_bytes=64)
         b_sb = f32_tile("b_sb", T)
-        for k, bank in enumerate(a_banks):
-            dst = a_sb[:, A_WIDTH * k : A_WIDTH * (k + 1)]
-            if k % 2 == 0:
-                nc.vector.tensor_copy(out=dst, in_=bank[:])
-            else:
-                nc.scalar.copy(out=dst, in_=bank[:])
+        nc.vector.tensor_copy(out=a_sb[:, : 2 * QUARTER], in_=a_head[:])
+        nc.scalar.copy(out=a_sb[:, 2 * QUARTER : 3 * QUARTER], in_=a_mid[:])
+        nc.vector.tensor_copy(out=a_sb[:, 3 * QUARTER :], in_=a_tail[:, :QUARTER])
+        nc.scalar.copy(out=b_sb[:, :QUARTER], in_=b_head[:])
 
-        cols = [slice(0, HALF), slice(HALF, SLOTS)]
-        ents = [slice(0, LIST_HALF), slice(LIST_HALF, 2 * LIST_HALF)]
+        b_rest = psum.tile([P, 2 * BANK], F32, name="b_rest", tag="a_then_b")
+        score_pass(b_rest[:, :QUARTER], qb_codes, qb_scales, QUARTER)
+        score_pass(b_rest[:, BANK:], qb_codes, qb_scales, 2 * QUARTER)
+
+        slots = [slice(0, HALF), slice(HALF, SLOTS)]
+        entries = [slice(0, HALF // GROUP), slice(HALF // GROUP, SLOTS // GROUP)]
 
         a1 = f32_tile("a1", SLOTS)
         d2 = f32_tile("d2", SLOTS)
@@ -132,30 +133,46 @@ def tile_attend_quotaratio_leaning_gated_heads_kernel(
         x2 = f32_tile("x2", SLOTS)
         x3 = f32_tile("x3", SLOTS)
         den = f32_tile("den", SLOTS)
-        nc.vector.tensor_copy(out=a1[:, cols[0]], in_=a_sb[:].indirect(list1[:, ents[0]]))
-        nc.scalar.activation(a1[:, cols[1]], a_sb[:].indirect(list1[:, ents[1]]), ACT.Copy)
-        for h in range(T // BANK):
-            nc.scalar.copy(out=b_sb[:, BANK * h : BANK * (h + 1)], in_=b_banks[h][:])
-        for h in (1, 0):
-            nc.vector.tensor_tensor(d2[:, cols[h]], a_sb[:].indirect(list2[:, ents[h]]), a1[:, cols[h]], ALU.subtract)
+        nc.vector.tensor_copy(out=a1[:, slots[0]], in_=a_sb[:].indirect(list1[:, entries[0]]))
+        nc.scalar.activation(a1[:, slots[1]], a_sb[:].indirect(list1[:, entries[1]]), ACT.Copy)
+        nc.scalar.copy(out=b_sb[:, QUARTER : 2 * QUARTER], in_=b_rest[:, :QUARTER])
+        nc.scalar.copy(out=b_sb[:, 2 * QUARTER :], in_=b_rest[:, BANK:])
+        for h in range(2):
+            nc.vector.tensor_tensor(
+                d2[:, slots[h]], a_sb[:].indirect(list2[:, entries[h]]), a1[:, slots[h]], ALU.subtract
+            )
         nc.scalar.activation(x2[:], d2[:], ACT.Exp)
         for h in range(2):
-            nc.vector.tensor_tensor(d3[:, cols[h]], b_sb[:].indirect(list3[:, ents[h]]), a1[:, cols[h]], ALU.subtract)
-            nc.scalar.activation(x3[:, cols[h]], d3[:, cols[h]], ACT.Exp)
+            nc.vector.tensor_tensor(
+                d3[:, slots[h]], b_sb[:].indirect(list3[:, entries[h]]), a1[:, slots[h]], ALU.subtract
+            )
+            nc.scalar.activation(x3[:, slots[h]], d3[:, slots[h]], ACT.Exp)
         for h in range(2):
             nc.vector.scalar_tensor_tensor(
-                den[:, cols[h]], x2[:, cols[h]], 1.0, x3[:, cols[h]], ALU.add, ALU.add
+                den[:, slots[h]], x2[:, slots[h]], 1.0, x3[:, slots[h]], ALU.add, ALU.add
             )
 
-        root = f32_tile("root", SLOTS)
-        s = f32_tile("s", SLOTS)
-        for h in range(2):
-            nc.scalar.activation(root[:, cols[h]], den[:, cols[h]], ACT.Abs_reciprocal_sqrt)
-            nc.vector.scalar_tensor_tensor(
-                s[:, cols[h]], root[:, cols[h]], lam_sb[:], root[:, cols[h]], ALU.mult, ALU.mult
-            )
+        by_vector, by_scalar = slice(0, RECIPROCAL_SLOTS), slice(RECIPROCAL_SLOTS, SLOTS)
+        inv_lam = f32_tile("inv_lam", 1)
+        inv_s = f32_tile("inv_s", SLOTS)
+        least0 = f32_tile("least0", 1)
+        least = f32_tile("least", 1)
+        top = f32_tile("top", 1)
         neg_max = f32_tile("neg_max", 1)
-        nc.vector.tensor_reduce(neg_max[:], s[:], AXIS.X, ALU.max, negate=True)
+        root = f32_tile("root", SLOTS - RECIPROCAL_SLOTS)
+        s = f32_tile("s", SLOTS)
+        nc.vector.reciprocal(inv_lam[:], lam_sb[:])
+        nc.vector.tensor_scalar(
+            inv_s[:, slots[0]], den[:, slots[0]], inv_lam[:], None, ALU.mult, ALU.min, accum_out=least0[:]
+        )
+        nc.vector.tensor_scalar(
+            inv_s[:, slots[1]], den[:, slots[1]], inv_lam[:], least0[:], ALU.mult, ALU.min, accum_out=least[:]
+        )
+        nc.scalar.activation(root[:], den[:, by_scalar], ACT.Abs_reciprocal_sqrt)
+        nc.vector.reciprocal(s[:, by_vector], inv_s[:, by_vector])
+        nc.vector.reciprocal(top[:], least[:])
+        nc.vector.tensor_scalar(neg_max[:], top[:], -1.0, None, ALU.mult)
+        nc.vector.scalar_tensor_tensor(s[:, by_scalar], root[:], lam_sb[:], root[:], ALU.mult, ALU.mult)
 
         lean_s = f32_tile("lean_s", SLOTS)
         gain128 = f32_tile("gain128", 1)
@@ -176,16 +193,16 @@ def tile_attend_quotaratio_leaning_gated_heads_kernel(
         nc.vector.scalar_tensor_tensor(psl[:], s[:], lean_sb[:], p[:], ALU.mult, ALU.mult, accum_out=psl_sum[:])
         nc.vector.tensor_scalar(factor[:], inv_sum[:], inv_sum[:], gain128[:], ALU.mult, ALU.mult)
 
-        w = f32_tile("w", SLOTS)
+        wz2 = f32_tile("wz2", SLOTS)
         gate = f32_tile("gate", SLOTS)
         result = f32_tile("result", SLOTS)
-        CH = 128
-        chunks = [slice(c, c + CH) for c in range(0, SLOTS, CH)]
+        chunks = [slice(c0, c0 + CHUNK) for c0 in range(0, SLOTS, CHUNK)]
         for c in chunks:
-            nc.vector.scalar_tensor_tensor(w[:, c], scaled[:, c], psl_sum[:], p[:, c], ALU.subtract, ALU.mult)
-            nc.scalar.activation(gate[:, c], w[:, c], ACT.Tanh, scale=factor[:])
-        for k, c in enumerate(chunks):
+            nc.vector.scalar_tensor_tensor(wz2[:, c], scaled[:, c], psl_sum[:], p[:, c], ALU.subtract, ALU.mult)
+            nc.scalar.activation(gate[:, c], wz2[:, c], ACT.Tanh, scale=factor[:])
+        stored = 0
+        for c in chunks:
             nc.vector.tensor_tensor(result[:, c], gate[:, c], base_sb[:, c], ALU.add)
-            if k >= 1:
-                st = slice(0, 2 * CH) if k == 1 else c
-                nc.sync.dma_start(out=out[:, st], in_=result[:, st])
+            if c.stop >= HALF:
+                nc.sync.dma_start(out=out[:, stored : c.stop], in_=result[:, stored : c.stop])
+                stored = c.stop

from contextlib import ExitStack

import concourse.mybir as mybir

D, T, SLOTS, Q = 512, 1024, 512, 128
FLOPS = 2 * 2 * D * T * Q

F32 = mybir.dt.float32
BF16 = mybir.dt.bfloat16
I32 = mybir.dt.int32
U32 = mybir.dt.uint32
U16 = mybir.dt.uint16
U8 = mybir.dt.uint8
FP8X4 = mybir.dt.float8_e4m3fn_x4
FP4X4 = mybir.dt.float4_e2m1fn_x4
ALU = mybir.AluOpType
ACT = mybir.ActivationFunctionType

P = 128
PACK = 4
QUADRANT = 32
SCALE_ROWS = 4
GROUP = 16
BANK = 512
QUARTER = T // 4
HALF = SLOTS // 2
VECTOR_QUERIES = 80
RECIPROCAL_SLOTS = 128
CHUNK = 128


def tile_attend_quotaratio_leaning_gated_heads_kernel(
    tc, query, query2, keys_words, keys_scales, lam, lean, base, gain2, offs, offs2, offs3, out
):
    nc = tc.nc
    with ExitStack() as ctx:
        sb = ctx.enter_context(tc.tile_pool(name="sb", bufs=1))
        psum = ctx.enter_context(tc.psum_pool(name="psum", bufs=1))

        def f32_tile(name, width):
            return sb.tile([P, width], F32, name=name, align_bytes=64)

        list1 = sb.tile([P, SLOTS // GROUP], U16, name="list1")
        list2 = sb.tile([P, SLOTS // GROUP], U16, name="list2")
        list3 = sb.tile([P, SLOTS // GROUP], U16, name="list3")
        qa_raw = sb.tile([P, PACK, Q], F32, name="qa_raw", align_bytes=64)
        qb_raw = sb.tile([P, PACK, Q], F32, name="qb_raw", tag="qb_then_a", align_bytes=64)
        key_words = sb.tile([P, 2 * T], U8, name="key_words", align_bytes=64)
        key_scales = sb.tile([P, T], U8, name="key_scales", align_bytes=64)
        lam_sb = f32_tile("lam_sb", 1)
        lean_sb = f32_tile("lean_sb", 1)
        gain_sb = f32_tile("gain_sb", 1)
        base_sb = f32_tile("base_sb", SLOTS)

        nc.vector.memset(key_scales[:].bitcast(I32), 0)
        nc.sync.dma_start(out=qa_raw[:], in_=query.rearrange("(p j) q -> p j q", j=PACK))
        nc.sync.dma_start(out=key_words[:].bitcast(I32), in_=keys_words[0].bitcast(I32))
        for quad in range(P // QUADRANT):
            nc.sync.dma_start(
                out=key_scales[QUADRANT * quad : QUADRANT * quad + SCALE_ROWS, :].bitcast(I32),
                in_=keys_scales[0, SCALE_ROWS * quad : SCALE_ROWS * (quad + 1), :].bitcast(I32),
            )
        nc.sync.dma_start(out=qb_raw[:], in_=query2.rearrange("(p j) q -> p j q", j=PACK))
        nc.sync.dma_start(list1[:], offs)
        nc.sync.dma_start(list2[:], offs2)
        nc.sync.dma_start(list3[:], offs3)
        nc.sync.dma_start(out=lam_sb[:], in_=lam)
        nc.sync.dma_start(out=lean_sb[:], in_=lean)
        nc.sync.dma_start(out=gain_sb[:], in_=gain2)
        nc.sync.dma_start(out=base_sb[:], in_=base)

        qa_bf = sb.tile([P, Q, PACK], BF16, name="qa_bf", align_bytes=64)
        qb_bf = sb.tile([P, Q, PACK], BF16, name="qb_bf", align_bytes=64)
        qa_codes = sb.tile([P, Q], U32, name="qa_codes", align_bytes=64)
        qb_codes = sb.tile([P, Q], U32, name="qb_codes", align_bytes=64)
        qa_scales = sb.tile([P, Q], U8, name="qa_scales", align_bytes=64)
        qb_scales = sb.tile([P, Q], U8, name="qb_scales", align_bytes=64)

        def round_and_interleave(grouped, raw):
            first, rest = slice(0, VECTOR_QUERIES), slice(VECTOR_QUERIES, Q)
            nc.vector.tensor_copy(out=grouped[:, first, :], in_=raw[:, :, first].rearrange("p j q -> p q j"))
            nc.scalar.copy(out=grouped[:, rest, :], in_=raw[:, :, rest].rearrange("p j q -> p q j"))

        def quantise(codes, scales, grouped):
            nc.vector.quantize_mx(
                out=codes[:].bitcast(FP8X4),
                scales=scales[:],
                in_=grouped[:].rearrange("p q j -> p (q j)"),
            )

        def score_pass(bank, codes, scales, t0):
            width = bank.shape[1]
            nc.tensor.matmul_mx(
                out=bank,
                lhsT=codes[:].bitcast(FP8X4),
                lhsT_scale=scales[:],
                rhs=key_words[:, 2 * t0 : 2 * (t0 + width)].bitcast(FP4X4),
                rhs_scale=key_scales[:, t0 : t0 + width],
                start=True,
                stop=True,
            )

        round_and_interleave(qa_bf, qa_raw)
        quantise(qa_codes, qa_scales, qa_bf)
        a_head = psum.tile([P, 2 * QUARTER], F32, name="a_head")
        a_mid = psum.tile([P, QUARTER], F32, name="a_mid")
        a_tail = psum.tile([P, 2 * BANK], F32, name="a_tail", tag="a_then_b")
        score_pass(a_head[:], qa_codes, qa_scales, 0)
        score_pass(a_mid[:], qa_codes, qa_scales, 2 * QUARTER)
        score_pass(a_tail[:, :QUARTER], qa_codes, qa_scales, 3 * QUARTER)
        round_and_interleave(qb_bf, qb_raw)
        quantise(qb_codes, qb_scales, qb_bf)
        b_head = psum.tile([P, QUARTER], F32, name="b_head")
        score_pass(b_head[:], qb_codes, qb_scales, 0)

        a_sb = sb.tile([P, T], F32, name="a_sb", tag="qb_then_a", align_bytes=64)
        b_sb = f32_tile("b_sb", T)
        nc.vector.tensor_copy(out=a_sb[:, : 2 * QUARTER], in_=a_head[:])
        nc.scalar.copy(out=a_sb[:, 2 * QUARTER : 3 * QUARTER], in_=a_mid[:])
        nc.vector.tensor_copy(out=a_sb[:, 3 * QUARTER :], in_=a_tail[:, :QUARTER])
        nc.scalar.copy(out=b_sb[:, :QUARTER], in_=b_head[:])

        b_rest = psum.tile([P, 2 * BANK], F32, name="b_rest", tag="a_then_b")
        score_pass(b_rest[:, :QUARTER], qb_codes, qb_scales, QUARTER)
        score_pass(b_rest[:, BANK:], qb_codes, qb_scales, 2 * QUARTER)

        slots = [slice(0, HALF), slice(HALF, SLOTS)]
        entries = [slice(0, HALF // GROUP), slice(HALF // GROUP, SLOTS // GROUP)]

        a1 = f32_tile("a1", SLOTS)
        d2 = f32_tile("d2", SLOTS)
        d3 = f32_tile("d3", SLOTS)
        x2 = f32_tile("x2", SLOTS)
        x3 = f32_tile("x3", SLOTS)
        den = f32_tile("den", SLOTS)
        nc.vector.tensor_copy(out=a1[:, slots[0]], in_=a_sb[:].indirect(list1[:, entries[0]]))
        nc.scalar.activation(a1[:, slots[1]], a_sb[:].indirect(list1[:, entries[1]]), ACT.Copy)
        nc.scalar.copy(out=b_sb[:, QUARTER : 2 * QUARTER], in_=b_rest[:, :QUARTER])
        nc.scalar.copy(out=b_sb[:, 2 * QUARTER :], in_=b_rest[:, BANK:])
        for h in range(2):
            nc.vector.tensor_tensor(
                d2[:, slots[h]], a_sb[:].indirect(list2[:, entries[h]]), a1[:, slots[h]], ALU.subtract
            )
        nc.scalar.activation(x2[:], d2[:], ACT.Exp)
        for h in range(2):
            nc.vector.tensor_tensor(
                d3[:, slots[h]], b_sb[:].indirect(list3[:, entries[h]]), a1[:, slots[h]], ALU.subtract
            )
            nc.scalar.activation(x3[:, slots[h]], d3[:, slots[h]], ACT.Exp)
        for h in range(2):
            nc.vector.scalar_tensor_tensor(
                den[:, slots[h]], x2[:, slots[h]], 1.0, x3[:, slots[h]], ALU.add, ALU.add
            )

        by_vector, by_scalar = slice(0, RECIPROCAL_SLOTS), slice(RECIPROCAL_SLOTS, SLOTS)
        inv_lam = f32_tile("inv_lam", 1)
        inv_s = f32_tile("inv_s", SLOTS)
        least0 = f32_tile("least0", 1)
        least = f32_tile("least", 1)
        top = f32_tile("top", 1)
        neg_max = f32_tile("neg_max", 1)
        root = f32_tile("root", SLOTS - RECIPROCAL_SLOTS)
        s = f32_tile("s", SLOTS)
        nc.vector.reciprocal(inv_lam[:], lam_sb[:])
        nc.vector.tensor_scalar(
            inv_s[:, slots[0]], den[:, slots[0]], inv_lam[:], None, ALU.mult, ALU.min, accum_out=least0[:]
        )
        nc.vector.tensor_scalar(
            inv_s[:, slots[1]], den[:, slots[1]], inv_lam[:], least0[:], ALU.mult, ALU.min, accum_out=least[:]
        )
        nc.scalar.activation(root[:], den[:, by_scalar], ACT.Abs_reciprocal_sqrt)
        nc.vector.reciprocal(s[:, by_vector], inv_s[:, by_vector])
        nc.vector.reciprocal(top[:], least[:])
        nc.vector.tensor_scalar(neg_max[:], top[:], -1.0, None, ALU.mult)
        nc.vector.scalar_tensor_tensor(s[:, by_scalar], root[:], lam_sb[:], root[:], ALU.mult, ALU.mult)

        lean_s = f32_tile("lean_s", SLOTS)
        gain128 = f32_tile("gain128", 1)
        nc.vector.tensor_scalar(lean_s[:], s[:], lean_sb[:], 1.0, ALU.mult, ALU.add)
        nc.vector.tensor_scalar(gain128[:], gain_sb[:], 128.0, None, ALU.mult)

        p = f32_tile("p", SLOTS)
        p_sum = f32_tile("p_sum", 1)
        nc.scalar.activation(p[:], s[:], ACT.Exp, bias=neg_max[:], accum_out=p_sum[:])

        psl = f32_tile("psl", SLOTS)
        psl_sum = f32_tile("psl_sum", 1)
        inv_sum = f32_tile("inv_sum", 1)
        factor = f32_tile("factor", 1)
        scaled = f32_tile("scaled", SLOTS)
        nc.scalar.activation(scaled[:], lean_s[:], ACT.Copy, scale=p_sum[:])
        nc.vector.reciprocal(inv_sum[:], p_sum[:])
        nc.vector.scalar_tensor_tensor(psl[:], s[:], lean_sb[:], p[:], ALU.mult, ALU.mult, accum_out=psl_sum[:])
        nc.vector.tensor_scalar(factor[:], inv_sum[:], inv_sum[:], gain128[:], ALU.mult, ALU.mult)

        wz2 = f32_tile("wz2", SLOTS)
        gate = f32_tile("gate", SLOTS)
        result = f32_tile("result", SLOTS)
        chunks = [slice(c0, c0 + CHUNK) for c0 in range(0, SLOTS, CHUNK)]
        for c in chunks:
            nc.vector.scalar_tensor_tensor(wz2[:, c], scaled[:, c], psl_sum[:], p[:, c], ALU.subtract, ALU.mult)
            nc.scalar.activation(gate[:, c], wz2[:, c], ACT.Tanh, scale=factor[:])
        stored = 0
        for c in chunks:
            nc.vector.tensor_tensor(result[:, c], gate[:, c], base_sb[:, c], ALU.add)
            if c.stop >= HALF:
                nc.sync.dma_start(out=out[:, stored : c.stop], in_=result[:, stored : c.stop])
                stored = c.stop
